import numpy as np, ml_dtypes
CORES = [48,51,52,55]
N = 4
BF = ml_dtypes.bfloat16
def gentries(a):
    return np.ascontiguousarray(a.reshape(8, 16, -1).transpose(0, 2, 1)).reshape(8, -1)
def gtable(e):
    e = np.asarray(e); return np.ascontiguousarray(e.reshape(8, -1, 16).transpose(0, 2, 1)).reshape(128, -1).astype(np.int32)
D, W, H, B, T = 3072, 3072, 4, 1, 2048
M = H * B
TOP = np.arange(16)[:, None]
def counts(rng, n):
    return np.minimum(M + ((96 - M) * rng.random((N, 8, 16, n)) ** rng.choice(np.array([1.0, 2.0, 4.0]), (N, 8, 1, n))).astype(np.int64), 95)
def lists(rng, n):
    return np.ascontiguousarray(np.argsort(rng.random((N, 8, M, n)), axis=-1)[..., :T])
def parts(rng):
    return (counts(rng, D), counts(rng, W), rng.integers(1, 4, (N, 8, 16, H)), lists(rng, D), lists(rng, W), rng.integers(0, 16, (N, 8, M, T)), rng.integers(0, 32, (N, 8, M, T)))
def near(p):
    t = p[:, :, 15:]; a = 32 * p[:, :, :15]; v = a // t; i = np.argmin(a - v * t, axis=2)[:, :, None]
    return np.take_along_axis(v, i, 2)[:, :, 0]
def pack(cd, cw, wt, dl, wl, zo, dr):
    b = lambda a, p: np.ascontiguousarray(a).reshape(N, p, -1).astype(np.float32).astype(BF)
    return {"nd": b(cd, 128), "nw": b(cw, 128), "wt": np.ascontiguousarray(wt).reshape(N, 128, H).astype(np.float32),
            "dl": np.stack([gtable(a.reshape(8, -1)) for a in dl]), "wl": np.stack([gtable(a.reshape(8, -1)) for a in wl]), "zo": b(zo, 8), "dr": b(dr, 8)}
def setup_inputs(rng):
    return pack(*parts(rng))
def setup_inputs_drain(rng):
    cd, cw, wt, dl, wl, zo, dr = parts(rng); s = (N, 8, M, T)
    u = np.argsort(rng.random((8, W)), axis=-1)[:, :T]; q = np.argsort(rng.random((N, 8, D)), axis=-1)[..., :T]; zeta = rng.integers(1, 16, (8, T))
    o = np.argsort(rng.random(s), axis=-1)
    dl = np.take_along_axis(np.broadcast_to(q[:, :, None], s), o, 3); wl = np.take_along_axis(np.broadcast_to(u[None, :, None], s), o, 3); zo = np.take_along_axis(np.broadcast_to(zeta[None, :, None], s), o, 3)
    dr[:, ::2] = 0
    for c, n in ((cd, D), (cw, W)):
        k = rng.integers(0, 4, (N, 4, 1, n))
        c[:, ::2] = np.where(k == 3, M + rng.integers(0, 2, (N, 4, 16, n)), np.where(k == 2, M, np.where(TOP == 0, 95, np.where(k == 0, M, c[:, ::2]))))
    i = dl[:, ::2, M - 1][:, :, None, :]; j = wl[:, ::2, M - 1][:, :, None, :]; z = zo[:, ::2, M - 1][:, :, None, :]
    more = 1 + (M - 1) * (TOP == 0) - M * (TOP == z)
    x = np.take_along_axis(cd[:, ::2], i, 3) + more; y = np.take_along_axis(cw[(np.arange(N) + H - 1) % N][:, ::2], j, 3) + more
    p = np.add.accumulate(x * y * wt[:, ::2, :, H - 1][..., None], axis=2)
    dr[:, ::2, M - 1] = np.where(rng.random((N, 4, T)) < 0.5, near(p), 0)
    return pack(cd, cw, wt, dl, wl, zo, dr)
def setup_inputs_ends(rng):
    cd, cw, wt, dl, wl, zo, dr = parts(rng)
    cd[:, 0] = 95; cw[:, 0] = 95; wt[:, 0] = 3; cd[:, 1] = M; cw[:, 1] = M; wt[:, 1] = 1
    dl[:, 2] = np.arange(T); wl[:, 2] = np.arange(W - T, W); dl[:, 3] = np.arange(D - 1, D - T - 1, -1); wl[:, 3] = np.arange(T - 1, -1, -1)
    dl[:, 4] = dl[:, 4, :1].copy(); wl[:, 4] = wl[:1, 4, :1].copy()
    for a, n in ((dl, D), (wl, W)):
        a[:, 5, :, 0] = (n - 1) * (np.arange(M) % 2); a[:, 5, :, T - 1] = (n - 1) * ((np.arange(M) + 1) % 2)
        a[:, 5, :, 1:T - 1] = 1 + np.argsort(rng.random((N, M, n - 2)), axis=-1)[..., :T - 2]
    zo[:, 1:4] = 15 * rng.integers(0, 2, (N, 3, M, T)); dr[:, 1:5] = 31 * rng.integers(0, 2, (N, 4, M, T))
    return pack(cd, cw, wt, dl, wl, zo, dr)
def setup_inputs_spread(rng):
    cd, cw, wt, dl, wl, zo, dr = parts(rng)
    cd, cw = [np.minimum(M + (np.exp2(7 * rng.random((N, 8, 1, n))) * rng.random((N, 8, 16, n))).astype(np.int64), 95) for n in (D, W)]
    wt = np.where(rng.random((N, 8, 16, H)) < rng.random((N, 8, 1, 1)), 1, wt)
    zo = np.minimum((16 * rng.random((N, 8, M, T)) ** np.exp2(rng.integers(-2, 3, (N, 8, M, 1)))).astype(np.int64), 15)
    dr = np.minimum((32 * rng.random((N, 8, M, T)) ** np.exp2(rng.integers(-2, 3, (N, 8, M, 1)))).astype(np.int64), 31)
    return pack(cd, cw, wt, dl, wl, zo, dr)
def setup_inputs_ties(rng):
    cd, cw, wt, dl, wl, zo, dr = parts(rng)
    zeta = rng.integers(0, 16, (1, 8, 1, 1)); up = (TOP == zeta).astype(np.int64)
    cd = rng.integers(M, 95, (N, 8, 1, D)) + up; cw = rng.integers(M, 95, (N, 8, 1, W)) + up
    wt = np.broadcast_to(rng.integers(1, 4, (N, 8, 1, H)), (N, 8, 16, H)); zo = np.broadcast_to(zeta, (N, 8, M, T))
    return pack(cd, cw, wt, dl, wl, zo, dr)
def setup_inputs_gaps(rng):
    cd, cw, wt, dl, wl, zo, dr = parts(rng); s = (N, 3, T)
    a = np.zeros((N, 3, 16, T), np.int64); b = np.zeros((N, 3, 16, T), np.int64)
    a[:, :, 15] = rng.integers(50, 55, s); b[:, :, 15] = rng.integers(50, 55, s)
    goal = 93 * a[:, :, 15] * b[:, :, 15] + rng.integers(-1, 2, s)
    sa = np.zeros((N, 3, 15, T), np.int64); sb = np.zeros((N, 3, 15, T), np.int64); rest = (goal - 7848) // 3
    for k in range(13):
        left = 13 - k; c = rng.integers(75, 96, s); n = (2 * rest + left * c) // (2 * left * c) if k < 12 else rest // c
        if k == 0: c, n = np.full(s, 95), np.full(s, 91)
        sa[:, :, k] = n; sb[:, :, k] = c; rest = rest - n * c
    rem = 7848 + (goal - 7848) % 3 + 3 * rest
    t = rem % 80; t = np.where(t < 9, t + 80, t)
    sa[:, :, 13] = t; sb[:, :, 13] = 81; sa[:, :, 14] = (rem - 81 * t) // 80; sb[:, :, 14] = 80
    flip = rng.random((N, 3, 1, T)) < 0.5; sa, sb = np.where(flip, sb, sa), np.where(flip, sa, sb)
    od = np.argsort(rng.random((N, 3, 15)), axis=-1); ix = np.broadcast_to(od[..., None], (N, 3, 15, T))
    np.put_along_axis(a, ix, sa, 2); np.put_along_axis(b, ix, sb, 2)
    wv = np.full((N, 3, 16), 3); np.put_along_axis(wv, od[..., 13:], 1, 2); wt[:, :3, :, 0] = wv
    up = (TOP == zo[:, :3, 0][:, :, None, :]).astype(np.int64)
    np.put_along_axis(cd[:, :3], dl[:, :3, 0][:, :, None, :], a - 1 + up, 3); np.put_along_axis(cw[:, :3], wl[:, :3, 0][:, :, None, :], b - 1 + up, 3)
    dr[:, :3, 0] = np.where(rng.random(s) < 0.75, 31, dr[:, :3, 0])
    o = np.argsort(rng.random((N, 2, M, T)), axis=-1)
    dl[:, 3:5] = o; wl[:, 3:5] = o - o % 16 + (5 * o + 3) % 16
    dl[:, 4] = D - 1 - dl[:, 4]; wl[:, 4] = W - 1 - wl[:, 4]
    for c, n in ((dl, D), (wl, W)):
        k = rng.random((N, 2, M, n)) - 2 * (np.arange(n) % 16 == rng.integers(0, 16, (N, 2, M, 1)))
        i = np.argsort(k, axis=-1)[..., :T]
        c[:, 5:7] = np.take_along_axis(i, np.argsort(rng.random(i.shape), axis=-1), 3)
    return pack(cd, cw, wt, dl, wl, zo, dr)
def check_inputs(d):
    bad = []
    for k, lo, hi in (("nd", M, 95), ("nw", M, 95), ("wt", 1, 3), ("dl", 0, D - 1), ("wl", 0, W - 1), ("zo", 0, 15), ("dr", 0, 31)):
        a = np.asarray(d[k]).astype(np.float64)
        if not (np.min(a) >= lo and np.max(a) <= hi): bad.append("range of " + k)
        if np.any(a != np.floor(a)): bad.append("whole numbers in " + k)
    for k in ("dl", "wl"):
        s = np.sort(np.stack([gentries(a) for a in d[k]]).reshape(N, 8, M, T), axis=-1)
        if np.any(s[..., 1:] == s[..., :-1]): bad.append("different numbers in a batch of " + k)
    return bad
def reference(nd, nw, wt, dl, wl, zo, dr):
    whole = lambda a: a.astype(np.float32).astype(np.int64)
    docs = whole(nd).reshape(N, 8, 16, D); blocks = whole(nw).reshape(N, 8, 16, W); weight = whole(wt).reshape(N, 8, 16, H)
    dls = np.stack([gentries(a) for a in dl]).astype(np.int64).reshape(N, 8, M, T); wls = np.stack([gentries(a) for a in wl]).astype(np.int64).reshape(N, 8, M, T)
    olds = whole(zo).reshape(N, 8, M, T); draws = whole(dr).reshape(N, 8, M, T); news = np.zeros((N, 8, M, T), np.int64)
    for h in range(H):
        who = (np.arange(N) + h) % N; mine = blocks[who]
        for b in range(B):
            m = h * B + b; di = dls[:, :, m][:, :, None, :]; wi = wls[:, :, m][:, :, None, :]
            old = (olds[:, :, m][:, :, None, :] == TOP).astype(np.int64)
            x = np.take_along_axis(docs, di, 3) - old; y = np.take_along_axis(mine, wi, 3) - old
            p = np.add.accumulate((x + 1) * (y + 1) * weight[:, :, :, h][..., None], axis=2)
            z = np.add.reduce((32 * p <= draws[:, :, m][:, :, None, :] * p[:, :, 15:]).astype(np.int64), axis=2)
            new = (z[:, :, None, :] == TOP).astype(np.int64)
            np.put_along_axis(docs, di, x + new, 3); np.put_along_axis(mine, wi, y + new, 3)
            news[:, :, m] = z
        blocks[who] = mine
    last = blocks[(np.arange(N) + H - 1) % N]
    return {"yd": docs.reshape(N, 128, D).astype(np.float32).astype(BF), "yw": last.reshape(N, 128, W).astype(np.float32).astype(BF), "yz": news.reshape(N, 8, M * T).astype(np.float32).astype(BF)}

from concourse.mybir import AluOpType as ALU, ActivationFunctionType as ACT

N, H, TOK, D = 4, 4, 2048, 3072
CUTS = [[0, 256, 768, 1280, 1792, 2048]] * 4
SPLIT = 512
BC_V = {(0, 0), (0, 1), (1, 0), (3, 3), (3, 4)}
NQ_A = {(2, 0), (2, 1), (2, 2), (2, 3), (3, 0), (3, 1), (3, 2), (3, 3)}
OUT = [(0, 1024, "a"), (1024, 2048, "a"), (2048, 3072, "v")]
SOFT_WAIT = True
ORDER = "Lz Ld0 Lw0 Lnw Lt Lnd Lr Lw1 Ld1 Lc gp p1 m1 m5 p3 gz gc Zb1_0 Zb0_0 Zb1_1 m4 p4 bg Zb1_2 p2 Nq1_0 Nq0_0 gx Zb0_2 Nq0_2 Zb0_1 Nq0_1 m3 t2 t1 t3 tw1 tw0 tw2 d1 p5 Zb0_3 Nq0_3 Zb1_3 Nq1_3 Vb0_3 Vb0_0 gi t4 ts d2 d3 d4 tv1 tv2 tv3 tv0 Cd0 Cw0 Ws F0 Nq1_1 Ga0_0 Ga0_1 X0_0 X0_1 Vb0_1 Gy0_1 Gy0_0 Y0_0 Ga0_2 X0_2 Gy0_2 Vb0_2 U0_0 T0_0 P0_0 Q0_0 Cw1 RL Cf0 Y0_1 U0_1 T0_1 P0_1 Q0_1 Nq1_2 Vb0_4 U0_2 T0_2 Sg0_0 Gy0_4 Cd1 Bn0_0 Bc0_0 Ac0_0 R0_0 Ga0_4 X0_4 Ga0_3 X0_3 Sg0_1 Bn0_1 Bc0_1 R0_1 Cf2 Cf1 Sd0_0 P0_2 Q0_2 Sg0_2 Y0_2 Vb1_2 Ac0_1 Sd0_1 Gy0_3 Y0_3 U0_3 P0_3 T0_3 Bn0_2 Bc0_2 R0_2 Q0_3 Sg0_3 p6 U0_4 T0_4 P0_4 Q0_4 Bn0_3 Sq Sw0_0 Sw0_1 Sg0_4 Bn0_4 Bc0_3 R0_3 Bc0_4 R0_4 Y0_4 Vb1_0 Ac0_2 Sd0_2 Ac0_3 Sd0_3 Vb1_1 Lq Ac0_4 Sd0_4 Ga1_0 X1_0 Ga1_1 y1 y2 y3 Zb2_1 Nq2_1 Zb2_0 Zb2_2 Nq2_2 Nq2_0 X1_1 Zb2_3 Nq2_3 Sw0_2 Sw0_3 Sw0_4 Gy1_0 U1_0 P1_0 Gy1_1 T1_0 Q1_0 U1_1 Sg1_0 P1_1 Bn1_0 T1_1 Q1_1 F1 Ga1_2 X1_2 Gy1_4 Y1_4 Ga1_3 X1_3 tw3 Bc1_0 R1_0 Ac1_0 Sg1_1 Bn1_1 Y1_0 Y1_1 Gy1_2 Y1_2 U1_2 T1_2 Bc1_1 R1_1 Ac1_1 P1_2 Q1_2 Ga1_4 Sd1_0 Sg1_2 Sd1_1 Vb1_3 Gy1_3 Y1_3 U1_3 T1_3 Vb1_4 X1_4 Zb3_3 Bn1_2 Bc1_2 R1_2 P1_3 Q1_3 Sg1_3 U1_4 T1_4 P1_4 Q1_4 Sw1_0 Sw1_1 Sg1_4 Bn1_3 Ac1_2 Zb3_0 Vb2_0 Bc1_3 R1_3 Ac1_3 Bn1_4 Bc1_4 Ac1_4 R1_4 Vb2_1 Nq3_3 Vb2_2 Sw1_2 Sw1_3 Sw1_4 F2 Gy2_0 Y2_0 Sd1_2 Zb3_2 Zb3_1 Sd1_3 Sd1_4 Ga2_0 X2_0 Ga2_1 X2_1 Ga2_2 U2_0 T2_0 P2_0 Q2_0 Gy2_1 Nq3_0 X2_2 Nq3_2 U2_1 T2_1 P2_1 Q2_1 Sg2_0 Bn2_0 Gy2_2 Y2_2 Ga2_4 X2_4 Gy2_4 Nq3_1 Vb2_3 Y2_1 Ga2_3 Bc2_0 R2_0 X2_3 U2_2 T2_2 Sg2_1 Bn2_1 Bc2_1 R2_1 Ac2_0 Sd2_0 P2_2 Q2_2 Vb2_4 Gy2_3 Y2_3 U2_3 T2_3 P2_3 Sg2_2 Bn2_2 Q2_3 Ac2_1 Sd2_1 U2_4 T2_4 P2_4 Q2_4 Sw2_0 Sw2_1 Bc2_2 Ac2_2 R2_2 Y2_4 Sg2_3 Bn2_3 Bc2_3 Ac2_3 R2_3 Sg2_4 Bn2_4 Bc2_4 R2_4 Ac2_4 Vb3_2 Sw2_2 Sw2_3 Vb3_1 Vb3_0 Vb3_3 Sd2_2 Sd2_3 Sd2_4 Ga3_0 X3_0 Ga3_1 X3_1 Ga3_2 X3_2 Ga3_3 Sw2_4 Gy3_0 U3_0 P3_0 Gy3_1 T3_0 Q3_0 Sg3_0 U3_1 P3_1 Gy3_2 Bn3_0 T3_1 Q3_1 U3_2 T3_2 X3_3 Bc3_0 Ga3_4 X3_4 Sg3_1 Bn3_1 Bc3_1 Gy3_4 P3_2 Q3_2 Vb3_4 Gy3_3 U3_3 Ac3_0 P3_3 Sd3_0 Sg3_2 Bn3_2 T3_3 Q3_3 Ac3_1 Sd3_1 U3_4 T3_4 Sw3_0 Sw3_1 Bc3_2 Ac3_2 P3_4 Q3_4 Sg3_3 Bn3_3 Bc3_3 Ac3_3 Z0_0 Z0_1 Sg3_4 Bn3_4 Bc3_4 Ac3_4 Sd3_2 Sd3_3 Sd3_4 Cv1 Od1 Cv0 Od0 Sw3_2 Sw3_3 Sw3_4 Wu1 Wu0 Ow1 Ow0 Wu2 Ow2 Cu2 Cv2 Od2 Z0_2 Z0_3 Z1_0 Z1_1 Z1_2 Z1_3 Z2_0 Z2_1 Z2_2 Z2_3 Z3_0 Z3_1 Z3_2 Z3_3 Zc Oz"

BF, F32 = "bfloat16", "float32"
SCRATCH = {name: ("sbuf", [rows, cols], kind) for name, rows, cols, kind in [
    ("w0", 128, D, BF), ("w1", 128, D, BF), ("w2", 128, D, BF), ("w3", 128, D, BF), ("wr", 128, D, BF),
    ("ndb", 128, D, BF), ("dw", 128, D, F32), ("yt", 128, D, BF), ("ydb", 128, D, BF),
    ("dl32", 128, 512, "int32"), ("wl32", 128, 512, "int32"), ("dl16", 128, 512, "uint16"), ("wl16", 128, 512, "uint16"), ("wn16", 128, 384, "uint16"),
    ("zo8", 16, 8192, BF), ("dr8", 8, 8192, BF), ("wts", 128, 4, F32), ("zc", 128, 512, BF), ("zq", 128, 512, BF), ("zs", 128, 512, BF),
    ("nq", 128, 8192, BF), ("ag", 128, TOK, BF), ("yy", 128, 8192, BF), ("yl", 128, 6144, BF), ("uu", 128, TOK, F32), ("uv", 128, TOK, F32),
    ("sg", 128, 8192, BF), ("an", 128, TOK, F32), ("bn", 128, 8192, BF), ("bl", 128, 6144, BF),
    ("ones", 128, 128, BF), ("ident", 128, 128, BF), ("xo", 128, 128, BF), ("zsel", 8, 128, BF), ("zsel2", 16, 128, BF), ("dm", 128, 128, BF),
    ("tri", 128, 128, F32), ("tot", 128, 128, F32), ("tw", 128, 1024, F32), ("big", 128, 144, BF), ("cols", 128, 144, F32),
    ("pint", 128, 8, "int32"), ("pand", 128, 8, "int32"), ("pf", 128, 8, F32)]}
SCRATCH.update({"pb%d" % b: ("psum", [128, 512], F32) for b in range(8)})

LOADS = ["Lc", "Lq", "Lz", "Lt", "Lr", "Ld0", "Lw0", "Lnd", "Lnw", "Ld1", "Lw1"]
STORES = ["Oz", "Ow0", "Ow1", "Ow2"] + ["Od%d" % k for k in range(len(OUT))]
REMOTE = ["RL"] + ["F%d" % h for h in range(H - 1)] + [k + "%d_%d" % (h, c) for k in "RY" for h in range(H - 1) for c in range(len(CUTS[h]) - 1)]
SEMAPHORES = ["c_pe", "c_v", "c_a", "c_g", "sent"] + LOADS + STORES + REMOTE
POOL = list(range(8))


def plan(g, T, send):
    ops = {}
    pe, v, a, sp = g.tensor, g.vector, g.scalar, g.sync
    P = lambda b: T["pb%d" % b]

    def op(name, q, fn, after=(), soft=(), far=(), bank=None, kind="c"):
        ops[name] = (q, kind, list(after), list(soft), list(far), bank, fn)

    def load(name, q, out, in_, after=()):
        op(name, q, lambda b: (a if q == "a" else sp).dma_start(out, in_), after, kind="dma")

    def sums(name, w, terms, after):
        def fn(b):
            for i, (l, r) in enumerate(terms):
                ins = pe.matmul(P(b)[:, 0:w], l, r, i == 0, i == len(terms) - 1)
            return ins
        op(name, "pe", fn, after, bank=("acq", name))

    def select(name, out, in_, pattern, cmp, fill, base, mult, after):
        op(name, "g", lambda b: g.affine_select(out, in_, pattern, cmp, fill, base, mult), after)

    load("Lz", "a", T.zo8[0:8, :], T.zo[:])
    load("Ld0", "sp", T.dl32[:, 0:128], T.dl[:, 0:128])
    load("Lw0", "a", T.wl32[:, 0:128], T.wl[:, 0:128])
    load("Lnd", "sp", T.ndb[:], T.nd[:])
    load("Lt", "a", T.wts[:], T.wt[:])
    load("Lnw", "sp", T.wr[:], T.nw[:])
    op("Ws", "v", lambda b: v.tensor_scalar(T.w0[:], T.wr[:], 1.0, 32.0, ALU.add, ALU.mult), ["Lnw"])
    load("Lr", "sp", T.dr8[:], T.dr[:])
    load("Lc", "sp", T.zc[:], T.zo[:])
    load("Ld1", "sp", T.dl32[:, 128:512], T.dl[:, 128:512])
    load("Lw1", "sp", T.wl32[:, 128:512], T.wl[:, 128:512])
    op("Sq", "a", lambda b: a.activation(T.zq[:], T.zc[:], ACT.Square), ["Lc"])
    load("Lq", "sp", T.zo8[8:16, :], T.zq[:], ["Sq"])
    op("Cd0", "v", lambda b: v.tensor_copy(T.dl16[:, 0:128], T.dl32[:, 0:128]), ["Ld0"])
    op("Cw0", "v", lambda b: v.tensor_copy(T.wl16[:, 0:128], T.wl32[:, 0:128]), ["Lw0"])
    op("Cd1", "v", lambda b: v.tensor_copy(T.dl16[:, 128:512], T.dl32[:, 128:512]), ["Ld1"])
    op("Cw1", "v", lambda b: v.tensor_copy(T.wl16[:, 128:512], T.wl32[:, 128:512]), ["Lw1"])

    op("m1", "v", lambda b: v.memset(T.ones[:], 1.0))
    op("m3", "v", lambda b: v.memset(T.tri[:], 1.0 / 32))
    op("m4", "v", lambda b: v.memset(T.tot[:], -1.0 / 1024))
    op("m5", "v", lambda b: v.memset(T.dm[:], 0.0))
    select("gz", T.zsel[:], T.ones[0:8, :], [[1, 8], [0, 16]], ALU.is_equal, 0.0, 0, -1, ["m1"])
    op("gp", "g", lambda b: g.iota(T.pint[:], [[0, 8]], 0, 1))
    op("p1", "v", lambda b: v.tensor_scalar(T.pand[:, 0:1], T.pint[:, 0:1], 15, None, ALU.bitwise_and), ["gp"])
    op("p2", "v", lambda b: v.tensor_copy(T.pf[:, 0:1], T.pand[:, 0:1]), ["p1"])
    op("p3", "v", lambda b: v.tensor_scalar(T.pand[:, 4:5], T.pint[:, 4:5], 7, None, ALU.bitwise_and), ["gp"])
    op("p4", "v", lambda b: v.tensor_scalar(T.pf[:, 4:5], T.pand[:, 4:5], 16.0, 15.0, ALU.mult, ALU.add), ["p3"])
    op("p5", "v", lambda b: v.tensor_scalar(T.pf[:, 1:2], T.pf[:, 0:1], T.pf[:, 0:1], -32.0, ALU.mult, ALU.mult), ["p2"])
    op("p6", "v", lambda b: v.tensor_scalar(T.pf[:, 2:3], T.pf[:, 1:2], 32.0, None, ALU.add), ["p5"])
    select("gi", T.ident[:], T.ones[:], [[-1, 128]], ALU.is_equal, 0.0, 0, 1, ["m1"])
    select("gx", T.xo[:], T.dm[:], [[-1, 128]], ALU.not_equal, -1.0, 0, 1, ["m5"])
    for h in range(H):
        op("tw%d" % h, "a", lambda b, h=h: a.activation(T.tw[:, 256 * h:256 * h + 128], T.tri[:], ACT.Copy, scale=T.wts[:, h:h + 1]), ["t3", "Lt"])
        op("tv%d" % h, "a", lambda b, h=h: a.activation(T.tw[:, 256 * h + 128:256 * h + 256], T.tot[:], ACT.Copy, scale=T.wts[:, h:h + 1]), ["ts", "Lt"])
    select("t1", T.tri[:, 8:128], T.tri[:, 8:128], [[1, 15], [16, 8]], ALU.is_ge, 0.0, 0, -1, ["m3"])
    select("t2", T.tri[:, 0:8], T.tri[:, 0:8], [[16, 8]], ALU.is_ge, 0.0, 15, -1, ["m3"])
    select("t3", T.tri[:], T.tri[:], [[0, 16], [-16, 8]], ALU.is_ge, 0.0, 0, 1, ["t1", "t2"])
    select("t4", T.tot[:], T.tot[:], [[0, 16], [16, 8]], ALU.is_ge, 0.0, 15, -1, ["m4"])
    select("ts", T.tot[:], T.tot[:], [[0, 16], [-16, 8]], ALU.is_ge, 0.0, 0, 1, ["t4"])
    select("d1", T.dm[:], T.dm[:], [[-1, 8], [-8, 16]], ALU.not_equal, -16.0, 0, 1, ["gx"])
    select("d2", T.dm[:], T.dm[:], [[-1, 8], [-8, 16]], ALU.not_equal, 16.0, -8, 1, ["d1"])
    select("d3", T.dm[0:8, :], T.dm[0:8, :], [[-1, 8], [-8, 16]], ALU.not_equal, 16.0, 0, 1, ["d2"])
    select("d4", T.dm[0:8, :], T.dm[0:8, :], [[-1, 8], [-8, 16]], ALU.not_equal, 16.0, 120, 1, ["d3"])
    op("y1", "g", lambda b: g.iota(T.zsel2[:], [[0, 8], [-2, 16]], 0, 0, allow_small_or_imprecise_dtypes=True))
    select("y2", T.zsel2[:], T.zsel2[:], [[-1, 8], [0, 16]], ALU.is_equal, 0.0, 0, 1, ["y1"])
    select("y3", T.zsel2[:], T.zsel2[:], [[-1, 8], [0, 16]], ALU.not_equal, 1.0, -8, 1, ["y2"])
    op("gc", "g", lambda b: g.iota(T.cols[:], [[1, 144]], 0, 0, allow_small_or_imprecise_dtypes=True))
    op("bg", "v", lambda b: v.tensor_scalar(T.big[:], T.cols[:], T.pf[:, 4:5], -0.5, ALU.is_equal, ALU.mult), ["gc", "p4"])

    for k in range(3):
        op("Cf%d" % k, "a", lambda b, k=k: a.activation(T.dw[:, 1024 * k:1024 * k + 1024], T.ndb[:, 1024 * k:1024 * k + 1024], ACT.Silu, bias=32.0, scale=32.0), ["Lnd"])

    op("RL", "g", lambda b: send("RL", T.wn16[:], T.wl16[:, 0:384]), ["Cw0", "Cw1"], kind="rem")
    W = [T.w0, T.w1, T.w2, T.w3]
    sd, sw = [], []
    for h in range(H):
        cuts = CUTS[h]; nc = len(cuts) - 1; o = h * TOK
        ready = sw[-1:] if h else ["Ws"]
        docs = sd[-1:] if h else ["Lnd"]
        sd, sw = [], []
        dl, wl = ("Cd0", "Cw0") if h == 0 else ("Cd1", "Cw1")
        if h < H - 1:
            op("F%d" % h, "g", lambda b, h=h: send("F%d" % h, W[h + 1][:], W[h][:]), ready, kind="rem")
        for k in range(4):
            s = slice(o + 512 * k, o + 512 * k + 512); n = "%d_%d" % (h, k); q = 4 * h + k
            if (h, k) in NQ_A:
                sums("Zb" + n, 512, [(T.zsel2[:], T.zo8[:, s])], ["y3", "Lz", "Lq"])
                op("Nq" + n, "a", lambda b, s=s: a.activation(T.nq[:, s], P(b)[:], ACT.Relu, bias=T.pf[:, 2:3], scale=-32.0), ["Zb" + n, "p6"], bank=("rel", "Zb" + n))
            else:
                sums("Zb" + n, 512, [(T.zsel[:], T.zo8[0:8, s])], ["gz", "Lz"])
                op("Nq" + n, "v", lambda b, s=s: v.tensor_scalar(T.nq[:, s], P(b)[:], T.pf[:, 0:1], 32.0, ALU.is_equal, ALU.mult), ["Zb" + n, "p2"], bank=("rel", "Zb" + n))
            op("Z" + n, "pe", lambda b, q=q, s=s: pe.matmul(P(b)[:], T.big[:, 15 - q:143 - q], T.sg[:, s], q == 0, q == 15),
               ["bg"] + ["Sg%d_%d" % (h, c) for c in range(nc) if cuts[c] < 512 * k + 512 and cuts[c + 1] > 512 * k],
               soft=["Z%d_%d" % ((q - 1) // 4, (q - 1) % 4)] if q else [], bank=("use" if q else "acq", "Z"))
        for c in range(nc):
            t0, t1 = cuts[c], cuts[c + 1]; w = t1 - t0; n = "%d_%d" % (h, c)
            nq = ["Nq%d_%d" % (h, k) for k in range(t0 // 512, (t1 - 1) // 512 + 1)]
            tok = slice(t0, t1); al = slice(o + t0, o + t1); cl = slice((o + t0) // 16, (o + t1) // 16)
            if h == 0:
                op("Ga" + n, "a", lambda b, tok=tok, cl=cl: a.activation(T.ag[:, tok], T.ndb[:, 0:D].indirect(T.dl16[:, cl]), ACT.Identity, bias=32.0, scale=32.0), [dl] + docs)
            else:
                op("Ga" + n, "a", lambda b, tok=tok, cl=cl: a.activation(T.ag[:, tok], T.dw[:, 0:D].indirect(T.dl16[:, cl]), ACT.Copy), [dl] + docs)
            sums("X" + n, w, [(T.xo[:], T.nq[:, al]), (T.ident[:], T.ag[:, tok])], ["gi", "gx", "Ga" + n] + nq)
            sums("Vb" + n, w, [(T.zsel[:], T.dr8[:, al])], ["gz", "Lr"])
            op("Gy" + n, "v", lambda b, h=h, al=al, cl=cl: v.tensor_tensor(T.yy[:, al], W[h][:, 0:D].indirect(T.wl16[:, cl]), T.nq[:, al], ALU.subtract), ready + [wl] + nq)
            op("U" + n, "v", lambda b, tok=tok, al=al, w=w: v.tensor_tensor(T.uu[:, tok], P(b)[:, 0:w], T.yy[:, al], ALU.mult), ["Gy" + n, "X" + n], bank=("use", "X" + n))
            op("T" + n, "v", lambda b, tok=tok, w=w: v.tensor_tensor(T.uv[:, tok], P(b)[:, 0:w], T.uu[:, tok], ALU.mult), ["U" + n, "Vb" + n], bank=("rel", "Vb" + n))
            op("P" + n, "pe", lambda b, h=h, tok=tok, w=w: pe.matmul(P(b)[:, 0:w], T.tw[:, 256 * h:256 * h + 128], T.uu[:, tok], True, False),
               ["U" + n, "tw%d" % h], bank=("acq", "D" + n))
            op("Q" + n, "pe", lambda b, h=h, tok=tok, w=w: pe.matmul(P(b)[:, 0:w], T.tw[:, 256 * h + 128:256 * h + 256], T.uv[:, tok], False, True),
               ["T" + n, "tv%d" % h], soft=["P" + n], bank=("use", "D" + n))
            op("Sg" + n, "a", lambda b, al=al, w=w: a.activation(T.sg[:, al], P(b)[:, 0:w], ACT.Sign, bias=-0.5), ["Q" + n], bank=("rel", "D" + n))
            sums("Bn" + n, w, [(T.dm[:], T.sg[:, al])], ["Sg" + n, "d4"])
            if (h, c) in BC_V:
                op("Bc" + n, "v", lambda b, al=al, w=w: v.tensor_copy(T.bn[:, al], P(b)[:, 0:w]), ["Bn" + n], bank=("rel", "Bn" + n))
            else:
                op("Bc" + n, "a", lambda b, al=al, w=w: a.activation(T.bn[:, al], P(b)[:, 0:w], ACT.Copy), ["Bn" + n], bank=("rel", "Bn" + n))
            op("Ac" + n, "v", lambda b, tok=tok, al=al, w=w: v.tensor_tensor(T.an[:, tok], P(b)[:, 0:w], T.bn[:, al], ALU.add), ["Bc" + n, "U" + n], bank=("rel", "X" + n))
            if h < H - 1:
                op("R" + n, "g", lambda b, n=n, al=al: send("R" + n, T.bl[:, al], T.bn[:, al]), ["Bc" + n], kind="rem")
                op("Y" + n, "g", lambda b, n=n, al=al: send("Y" + n, T.yl[:, al], T.yy[:, al]), ["Gy" + n], kind="rem")
            for u0 in range(t0, t1, SPLIT):
                u1 = min(u0 + SPLIT, t1); cols = slice((o + u0) // 16, (o + u1) // 16); s = slice(o + u0, o + u1)
                e = "%d_%d" % (h, len(sd))
                op("Sd" + e, "a", lambda b, cols=cols, u0=u0, u1=u1: a.activation(T.dw[:, 0:D].indirect(T.dl16[:, cols]), T.an[:, u0:u1], ACT.Silu), ["Ac" + n],
                   soft=sd[-1:] or (["Ga%d_%d" % (h, j) for j in range(nc)] if h else ["Cf0", "Cf1", "Cf2"]))
                if h < H - 1:
                    op("Sw" + e, "v", lambda b, h=h, cols=cols, s=s: v.tensor_tensor(W[h + 1][:, 0:D].indirect(T.wn16[:, cols]), T.yl[:, s], T.bl[:, s], ALU.add),
                       soft=sw[-1:], far=["RL", "F%d" % h, "Y" + n, "R" + n])
                else:
                    op("Sw" + e, "v", lambda b, h=h, cols=cols, s=s: v.tensor_tensor(W[h][:, 0:D].indirect(T.wl16[:, cols]), T.yy[:, s], T.bn[:, s], ALU.add), ["Bc" + n],
                       soft=sw[-1:] or ["Gy%d_%d" % (h, j) for j in range(nc)])
                sd.append("Sd" + e); sw.append("Sw" + e)

    op("Zc", "v", lambda b: v.tensor_scalar(T.zs[:], P(b)[:], 8.0, None, ALU.add), ["Z3_3"], bank=("rel", "Z"))
    load("Oz", "sp", T.yz[:], T.zs[:], ["Zc"])
    for k in range(3):
        s = slice(1024 * k, 1024 * k + 1024)
        op("Wu%d" % k, "v", lambda b, s=s: v.tensor_scalar(T.wr[:, s], T.w3[:, s], 1.0 / 32, -1.0, ALU.mult, ALU.add), sw[-1:])
        load("Ow%d" % k, "sp", T.yw[:, s], T.wr[:, s], ["Wu%d" % k])
    for k, (s0, s1, q) in enumerate(OUT):
        if q == "v":
            op("Cu%d" % k, "v", lambda b, s0=s0, s1=s1: v.tensor_copy(T.yt[:, s0:s1], T.dw[:, s0:s1]), sd[-1:])
            op("Cv%d" % k, "v", lambda b, s0=s0, s1=s1: v.tensor_scalar(T.ydb[:, s0:s1], T.yt[:, s0:s1], 1.0 / 32, -1.0, ALU.mult, ALU.add), ["Cu%d" % k])
        else:
            op("Cv%d" % k, "a", lambda b, s0=s0, s1=s1: a.activation(T.ydb[:, s0:s1], T.dw[:, s0:s1], ACT.Relu, bias=-1.0005, scale=1.0 / 32), sd[-1:])
        load("Od%d" % k, "sp", T.yd[:, s0:s1], T.ydb[:, s0:s1], ["Cv%d" % k])
    return ops


def resolve(ops, order):
    free = list(POOL); held = {}; last = {}; out = []
    for name in order:
        q, kind, after, soft, far, bank, fn = ops[name]
        b = None
        need = list(after) + [s for s in soft if (SOFT_WAIT and q != "pe") or ops[s][0] != q]
        if bank is not None:
            if bank[0] == "acq":
                held[bank[1]] = free.pop(0)
            b = held[bank[1]]
            if bank[0] == "rel":
                free.append(b)
            seen = last.setdefault(b, {})
            need += [s for e, s in seen.items() if e != q]
            seen[q] = name
        out.append((name, b, need))
    return out


def rank_program(g, core, T, topo):
    rank = T.rank_of(core)
    if rank is None:
        return
    dst = T.cores[(rank - 1) % N]; src = T.cores[(rank + 1) % N]
    rid, pid, _ = topo.addr(dst)
    out_n = len(topo.engines(core, dst)); in_n = len(topo.engines(src, core))

    def send(name, out, in_):
        return g.remote_dma(out, in_, T.sem[name], T.sem.sent, pid, rid, topo.mask(core, dst))

    ops = plan(g, T, send)
    queue = {"pe": g.tensor, "v": g.vector, "a": g.scalar, "g": g, "sp": g.sync}
    known = {q: {} for q in queue}; count = {q: 0 for q in queue}; done = {}; total = {"sent": 0}; waited = {}

    def wait(q, sem, val, implies):
        if known[q].get(sem, 0) < val:
            queue[q].wait_ge(T.sem[sem], val)
            waited[sem] = max(waited.get(sem, 0), val)
            known[q][sem] = val
            for s, x in implies.items():
                if known[q].get(s, 0) < x:
                    known[q][s] = x

    steps = resolve(ops, ORDER.split())
    place = {name: i for i, (name, _, _) in enumerate(steps)}
    for name, b, need in steps:
        q, kind, _, _, far, _, fn = ops[name]
        for s in sorted(set(need), key=lambda s: -place[s]):
            wait(q, *done[s])
        for s in far:
            wait(q, s, in_n, {})
        ins = fn(b)
        if kind == "c":
            count[q] += 1
            ins.then_inc(T.sem["c_" + q], 1)
            done[name] = ("c_" + q, count[q], dict(known[q])); total["c_" + q] = count[q]
        elif kind == "dma":
            ins.then_inc(T.sem[name], 16)
            done[name] = (name, 16, dict(known[q])); total[name] = 16
        else:
            total["sent"] += out_n
    for sem, val in total.items():
        if waited.get(sem, 0) < val:
            g.wait_ge(T.sem[sem], val)
